import numpy as np
import ml_dtypes


def mxq(x, axis, fmt="e4m3"):
    dtype, down = {"e4m3": (ml_dtypes.float8_e4m3fn, 7), "e5m2": (ml_dtypes.float8_e5m2, 14)}[fmt]
    v = np.moveaxis(np.asarray(x, np.float32).astype(ml_dtypes.bfloat16).astype(np.float64), axis, -1)
    blocks = v.reshape(v.shape[:-1] + (-1, 32))
    amax = np.abs(blocks).max(-1, keepdims=True)
    byte = np.maximum(np.where(amax > 0, np.frexp(amax)[1] - 1 + 127, 0) - down, 1)
    scale = np.exp2(byte - 127.0)
    codes = (blocks / scale).astype(np.float32).astype(dtype).astype(np.float64)
    return np.moveaxis((codes * scale).reshape(v.shape), -1, axis)


WIDE = False


def mx_kscale(k):
    if not WIDE:
        return np.ones(k)
    levels = np.array([10, -10, 5, -5, 0])
    if k % 512:
        return np.exp2(np.random.permutation(np.resize(levels, k // 32))).repeat(32)
    a = np.empty((k // 512, 16))
    for p in range(k // 512):
        a[p, :8] = np.random.permutation(np.resize(levels, 8))
        for g in range(8):
            far = levels[np.abs(levels - a[p, g]) >= 10]
            a[p, g + 8] = far[np.random.randint(len(far))]
    return np.exp2(a.ravel()).repeat(32)


def f64(x):
    return np.asarray(x).astype(np.float64)


def striped(idx):
    return np.tile(np.asarray(idx).reshape(-1, 16).T, (8, 1)).astype(np.uint16)


def unstriped(offs):
    return offs[:16].T.reshape(-1).astype(np.int64)


E2M1 = np.array([0.0, 0.5, 1.0, 1.5, 2.0, 3.0, 4.0, 6.0, -0.0, -0.5, -1.0, -1.5, -2.0, -3.0, -4.0, -6.0])


def pack_weight(w, fmt):
    k, n = w.shape
    w = f64(np.asarray(w, np.float32).astype(ml_dtypes.bfloat16)).reshape(k // 32, 32, n)
    amax = np.abs(w).max(1)
    if fmt == "e4m3":
        byte = np.frexp(amax)[1] - 1 + 127 - 7
    else:
        mant, ex = np.frexp(amax / 6.0)
        byte = np.where(mant > 0.5, ex, ex - 1) + 127
    byte = np.clip(np.where(amax > 0, byte, 1), 1, 254)
    scaled = (w * np.exp2(127.0 - byte)[:, None, :]).reshape(k, n).astype(np.float32)
    by_word = np.ascontiguousarray(scaled.reshape(k // 512, 128, 4, n).transpose(0, 1, 3, 2))
    if fmt == "e4m3":
        words = by_word.astype(ml_dtypes.float8_e4m3fn).view(np.uint8)
    else:
        c = by_word.astype(ml_dtypes.float4_e2m1fn).view(np.uint8) & 0xF
        words = (c[..., 0::2] | (c[..., 1::2] << 4)).reshape(k // 512, 128, 2 * n)
    return np.ascontiguousarray(words), np.ascontiguousarray(byte.astype(np.uint8).reshape(k // 512, 16, n))


def unpack_weight(words, scales, fmt):
    g, _, n = scales.shape
    words = np.ascontiguousarray(words).reshape(g, 128, n, -1)
    if fmt == "e4m3":
        vals = words.view(ml_dtypes.float8_e4m3fn).astype(np.float64)
    else:
        nib = np.empty((g, 128, n, 4), np.uint8)
        nib[..., 0::2] = words & 0xF
        nib[..., 1::2] = words >> 4
        vals = E2M1[nib]
    vals = vals * np.repeat(np.exp2(scales.astype(np.float64) - 127.0), 8, axis=1)[..., None]
    return vals.transpose(0, 1, 3, 2).reshape(g * 512, n)


D, T, R, I, Q, E = 512, 2048, 1024, 512, 128, 512


def setup_inputs():
    n = np.random.standard_normal
    idx = np.random.permutation(T)[:R]
    idx2 = np.random.permutation(R)[:I]
    fd = mx_kscale(D)
    fi = mx_kscale(I)
    keysp = pack_weight(n((D, T)) / fd[:, None], "e4m3")
    return {
        "query": (n((D, Q)) * 0.25 / np.sqrt(D) * fd[:, None]).astype(np.float32),
        "keys_words": keysp[0],
        "keys_scales": keysp[1],
        "size": (np.random.uniform(0.5, 2.0, (1, I)) * fi).astype(np.float32),
        "vals": (n((E, T))).astype(np.float32),
        "vsc": (np.random.uniform(0.5, 2.0, (I, 1)) / fi[:, None]).astype(np.float32),
        "offs": striped(idx),
        "offs2": striped(idx2),
    }


def reference(query, keys_words, keys_scales, size, vals, vsc, offs, offs2):
    idx = unstriped(offs)
    idx2 = unstriped(offs2)
    keysu = unpack_weight(keys_words, keys_scales, "e4m3")
    queryq = mxq(f64(query), 0, "e4m3")
    keysidxg = keysu[:, idx]
    a = queryq.T @ keysidxg
    s = a[:, idx2] * 1.5
    p = np.exp(s - np.max(s, axis=1, keepdims=True))
    w = p * f64(size) / np.sum(p, axis=1, keepdims=True)
    wt = w.T
    vr = np.maximum(f64(vals)[:, idx], 0.0)
    vt = vr[:, idx2].T
    vv = vt * f64(vsc)
    wtq = mxq(wt, 0, "e4m3")
    vvq = mxq(vv, 0, "e4m3")
    o = wtq.T @ vvq
    return o

@@ -1,0 +1,210 @@
+from contextlib import ExitStack
+
+import concourse.mybir as mybir
+
+D, T, R, I, Q, E = 512, 2048, 1024, 512, 128, 512
+FLOPS = 2 * D * Q * R + 2 * I * Q * E
+
+F32 = mybir.dt.float32
+BF16 = mybir.dt.bfloat16
+I32 = mybir.dt.int32
+U32 = mybir.dt.uint32
+U16 = mybir.dt.uint16
+U8 = mybir.dt.uint8
+FP8X4 = mybir.dt.float8_e4m3fn_x4
+ALU = mybir.AluOpType
+ACT = mybir.ActivationFunctionType
+
+P = 128
+PACK = 4
+BANK = 512
+SLOT = 4 * T
+HALF = R // 2
+PIECE = 4 * HALF
+
+
+def tile_attend_residentset_kernel(tc, query, keys_words, keys_scales, size, vals, vsc, offs, offs2, out):
+    nc = tc.nc
+    with ExitStack() as ctx:
+        keep = ctx.enter_context(tc.tile_pool(name="keep", bufs=1))
+        shared = ctx.enter_context(tc.tile_pool(name="shared", bufs=1))
+        psum = ctx.enter_context(tc.psum_pool(name="psum", bufs=1))
+        turn = ctx.enter_context(tc.psum_pool(name="turn", bufs=3))
+
+        def tenant(at, name, shape, dtype):
+            return shared.tile(shape, dtype, name=name, offset=at, align_bytes=64)
+
+        def own(name, shape, dtype):
+            return keep.tile(shape, dtype, name=name, align_bytes=64)
+
+        idx = keep.tile([P, R // 16], U16, name="idx")
+        idx2 = keep.tile([P, I // 16], U16, name="idx2")
+        ident = own("ident", [P, P], F32)
+        key_bytes = own("key_bytes", [P, T], U8)
+        ones = tenant(SLOT - 256, "ones", [P, P], F32)
+        q_raw = own("q_raw", [P, PACK, Q], F32)
+
+        nc.vector.memset(key_bytes[:].bitcast(I32), 0)
+        nc.gpsimd.memset(ones[:], 1.0)
+        nc.gpsimd.affine_select(
+            out=ident[:], in_=ones[:], compare_op=ALU.is_equal, fill=0.0, base=0, pattern=[[-1, P]], channel_multiplier=1
+        )
+        nc.sync.dma_start(idx[:], offs)
+        nc.sync.dma_start(q_raw[:], query.rearrange("(p t) q -> p t q", t=PACK))
+        nc.sync.dma_start(idx2[:], offs2)
+        for g in range(4):
+            nc.sync.dma_start(key_bytes[32 * g : 32 * g + 4, :].bitcast(I32), keys_scales[0, 4 * g : 4 * g + 4, :].bitcast(I32))
+        key_words = tenant(0, "key_words", [P, T], U32)
+        nc.sync.dma_start(key_words[:].bitcast(I32), keys_words[0].rearrange("p n t -> p (n t)").bitcast(I32))
+
+        def load_vals(c, slot):
+            pool_rows = tenant(slot, "vals%d" % c, [P, T], F32)
+            nc.sync.dma_start(pool_rows[:], vals[c * P : (c + 1) * P, :])
+            return pool_rows
+
+        vals0 = load_vals(0, SLOT)
+        q_bf = own("q_bf", [P, Q, PACK], BF16)
+        q_codes = tenant(4 * SLOT, "q_codes", [P, Q], U32)
+        q_scales = own("q_scales", [P, Q], U8)
+        nc.scalar.copy(q_bf[:], q_raw[:].rearrange("p t q -> p q t"))
+
+        halves = [slice(h * HALF, (h + 1) * HALF) for h in range(2)]
+        idx_halves = [idx[:, h * HALF // 16 : (h + 1) * HALF // 16] for h in range(2)]
+
+        kg_words = tenant(2 * SLOT, "kg_words", [P, R], U32)
+        kg_bytes = tenant(3 * SLOT, "kg_bytes", [P, R], U8)
+        nc.vector.tensor_copy(kg_bytes[:], key_bytes[:].indirect(idx[:]))
+        nc.vector.quantize_mx(out=q_codes[:].bitcast(FP8X4), scales=q_scales[:], in_=q_bf[:].rearrange("p q t -> p (q t)"))
+        a = own("a", [P, R], F32)
+        for h in range(2):
+            nc.vector.tensor_copy(kg_words[:, halves[h]], key_words[:].indirect(idx_halves[h]))
+            score_bank = psum.tile([P, HALF], F32, name="score_bank%d" % h)
+            nc.tensor.matmul_mx(
+                out=score_bank[:], lhsT=q_codes[:].bitcast(FP8X4), lhsT_scale=q_scales[:],
+                rhs=kg_words[:, halves[h]].bitcast(FP8X4), rhs_scale=kg_bytes[:, halves[h]], start=True, stop=True,
+            )
+            nc.scalar.copy(a[:, halves[h]], score_bank[:])
+        vsc_col = tenant(0, "vsc_col", [P, PACK], F32)
+        nc.sync.dma_start(vsc_col[:], vsc.rearrange("(p t) o -> p (t o)", t=PACK))
+        size_col = tenant(64, "size_col", [P, PACK], F32)
+        nc.sync.dma_start(size_col[:], size.rearrange("o (p t) -> (o p) t", t=PACK))
+        vals1 = load_vals(1, 2 * SLOT)
+        vals2 = load_vals(2, 3 * SLOT)
+        vals3 = load_vals(3, 4 * SLOT)
+
+        def resident(c, pool_rows, places):
+            vr = own("vr%d" % c, [P, R], F32)
+            for h in range(2):
+                picked = tenant(places[h], "picked%d_%d" % (c, h), [P, HALF], F32)
+                nc.vector.tensor_copy(picked[:], pool_rows[:].indirect(idx_halves[h]))
+                nc.scalar.activation(vr[:, halves[h]], picked[:], ACT.Relu)
+            return vr
+
+        def look_up(window, found):
+            nc.vector.tensor_copy(found[:], window[:].indirect(idx2[:]))
+
+        def turned(rows):
+            bank = turn.tile([P, PACK, P], F32, name="bank")
+            for t in range(PACK):
+                nc.tensor.transpose(bank[:, t, :], rows[:, t : I : PACK], ident[:])
+            return bank
+
+        def scale(bank, factor, planes):
+            for t in range(PACK):
+                nc.scalar.activation(planes[:, t, :], bank[:, t, :], ACT.Copy, scale=factor[:, t : t + 1])
+
+        def weave(planes, woven):
+            nc.scalar.copy(woven, planes[:].rearrange("p t n -> p n t"))
+
+        def quantise(woven, codes, scales):
+            nc.vector.quantize_mx(out=codes[:].bitcast(FP8X4), scales=scales[:], in_=woven[:].rearrange("p n t -> p (n t)"))
+
+        def product(c0, codes, scales, evac):
+            width = codes.shape[1]
+            out_bank = psum.tile([P, width], F32, name="out_bank%d" % c0)
+            staged = own("staged%d" % c0, [P, width], F32)
+            nc.tensor.matmul_mx(
+                out=out_bank[:], lhsT=w_codes[:].bitcast(FP8X4), lhsT_scale=w_scales[:],
+                rhs=codes[:].bitcast(FP8X4), rhs_scale=scales[:], start=True, stop=True,
+            )
+            evac(staged[:], out_bank[:])
+            nc.sync.dma_start(out[:, c0 * P : c0 * P + width], staged[:])
+
+        FOUND, PLANES, WOVEN = [P, I], [P, PACK, P], [P, P, PACK]
+        base = 5 * SLOT
+        at0, at1, at2, at3 = base, base + 2 * PIECE, base + 5 * PIECE, base + 8 * PIECE
+
+        vr0 = resident(0, vals0, (at0, at0 + PIECE))
+        a_step = tenant(at0, "a_step", FOUND, F32)
+        look_up(a, a_step)
+        neg_s = own("neg_s", FOUND, F32)
+        neg_max = own("neg_max", [P, 1], F32)
+        p = own("p", FOUND, F32)
+        p_sum = own("p_sum", [P, 1], F32)
+        nc.vector.tensor_scalar(neg_s[:], a_step[:], -1.5, None, ALU.mult, ALU.min, accum_out=neg_max[:])
+        nc.scalar.activation(p[:], neg_s[:], ACT.Exp, bias=neg_max[:], scale=-1.0, accum_out=p_sum[:])
+        vt0 = own("vt0", FOUND, F32)
+        look_up(vr0, vt0)
+        inv_sum = own("inv_sum", [P, 1], F32)
+        nc.vector.reciprocal(inv_sum[:], p_sum[:])
+        p_norm = own("p_norm", FOUND, F32)
+        nc.scalar.activation(p_norm[:], p[:], ACT.Copy, scale=inv_sum[:])
+        planes0 = own("planes0", PLANES, BF16)
+        scale(turned(vt0), vsc_col, planes0)
+        bank_w = turned(p_norm)
+
+        vr1 = resident(1, vals1, (at1, at1 + PIECE))
+        woven01 = tenant(2 * SLOT, "woven01", [P, 2 * P, PACK], BF16)
+        weave(planes0, woven01[:, 0:P, :])
+
+        vr2 = own("vr2", [P, R], F32)
+        picked2_0 = tenant(at2, "picked2_0", [P, HALF], F32)
+        picked2_1 = own("picked2_1", [P, HALF], F32)
+        nc.vector.tensor_copy(picked2_0[:], vals2[:].indirect(idx_halves[0]))
+        nc.scalar.activation(vr2[:, halves[0]], picked2_0[:], ACT.Relu)
+        nc.vector.tensor_copy(picked2_1[:], vals2[:].indirect(idx_halves[1]))
+        planes_w = tenant(3 * SLOT, "planes_w", PLANES, BF16)
+        scale(bank_w, size_col, planes_w)
+        nc.scalar.activation(vr2[:, halves[1]], picked2_1[:], ACT.Relu)
+        woven_w = own("woven_w", WOVEN, BF16)
+        weave(planes_w, woven_w[:])
+
+        vt1 = tenant(at2 - PIECE // 2, "vt1", FOUND, F32)
+        look_up(vr1, vt1)
+        bank1 = turned(vt1)
+
+        vr3 = resident(3, vals3, (at2 + PIECE // 2, at3))
+        planes1 = tenant(4 * SLOT, "planes1", PLANES, BF16)
+        scale(bank1, vsc_col, planes1)
+        weave(planes1, woven01[:, P : 2 * P, :])
+        vt2 = tenant(at2 + PIECE // 2, "vt2", FOUND, F32)
+        look_up(vr2, vt2)
+        vt3 = own("vt3", FOUND, F32)
+        look_up(vr3, vt3)
+
+        w_codes = tenant(at3, "w_codes", [P, Q], U32)
+        w_scales = own("w_scales", [P, Q], U8)
+        quantise(woven_w, w_codes, w_scales)
+        codes01 = tenant(at3 + 4 * Q, "codes01", [P, 2 * P], U32)
+        scales01 = own("scales01", [P, 2 * P], U8)
+        quantise(woven01, codes01, scales01)
+
+        woven2 = own("woven2", WOVEN, BF16)
+        planes2 = own("planes2", PLANES, BF16)
+        scale(turned(vt2), vsc_col, planes2)
+        weave(planes2, woven2[:])
+        bank3 = turned(vt3)
+        product(0, codes01, scales01, nc.scalar.copy)
+
+        woven3 = own("woven3", WOVEN, BF16)
+        nc.vector.tensor_tensor(
+            woven3[:], bank3[:].rearrange("p t n -> p n t"), vsc_col[:].unsqueeze(1).to_broadcast([P, P, PACK]), ALU.mult
+        )
+        codes2 = own("codes2", [P, P], U32)
+        scales2 = own("scales2", [P, P], U8)
+        quantise(woven2, codes2, scales2)
+        codes3 = own("codes3", [P, P], U32)
+        scales3 = own("scales3", [P, P], U8)
+        quantise(woven3, codes3, scales3)
+        product(2, codes2, scales2, nc.scalar.copy)
+        product(3, codes3, scales3, nc.vector.tensor_copy)

@@ -45,7 +45,7 @@ def tile_attend_residentset_kernel(tc, query, keys_words, keys_scales, size, val
         q_raw = own("q_raw", [P, PACK, Q], F32)
 
         nc.vector.memset(key_bytes[:].bitcast(I32), 0)
-        nc.gpsimd.memset(ones[:], 1.0)
+        nc.vector.memset(ones[:], 1.0)
         nc.gpsimd.affine_select(
             out=ident[:], in_=ones[:], compare_op=ALU.is_equal, fill=0.0, base=0, pattern=[[-1, P]], channel_multiplier=1
         )
@@ -88,8 +88,8 @@ def tile_attend_residentset_kernel(tc, query, keys_words, keys_scales, size, val
         nc.sync.dma_start(vsc_col[:], vsc.rearrange("(p t) o -> p (t o)", t=PACK))
         size_col = tenant(64, "size_col", [P, PACK], F32)
         nc.sync.dma_start(size_col[:], size.rearrange("o (p t) -> (o p) t", t=PACK))
-        vals1 = load_vals(1, 2 * SLOT)
-        vals2 = load_vals(2, 3 * SLOT)
+        vals1 = load_vals(2, 2 * SLOT)
+        vals2 = load_vals(1, 3 * SLOT)
         vals3 = load_vals(3, 4 * SLOT)
 
         def resident(c, pool_rows, places):
@@ -117,15 +117,15 @@ def tile_attend_residentset_kernel(tc, query, keys_words, keys_scales, size, val
             nc.scalar.copy(woven, planes[:].rearrange("p t n -> p n t"))
 
         def quantise(woven, codes, scales):
-            nc.vector.quantize_mx(out=codes[:].bitcast(FP8X4), scales=scales[:], in_=woven[:].rearrange("p n t -> p (n t)"))
+            nc.vector.quantize_mx(out=codes.bitcast(FP8X4), scales=scales, in_=woven[:].rearrange("p n t -> p (n t)"))
 
         def product(c0, codes, scales, evac):
             width = codes.shape[1]
             out_bank = psum.tile([P, width], F32, name="out_bank%d" % c0)
             staged = own("staged%d" % c0, [P, width], F32)
             nc.tensor.matmul_mx(
-                out=out_bank[:], lhsT=w_codes[:].bitcast(FP8X4), lhsT_scale=w_scales[:],
-                rhs=codes[:].bitcast(FP8X4), rhs_scale=scales[:], start=True, stop=True,
+                out=out_bank[:], lhsT=early_codes[:, 0:Q].bitcast(FP8X4), lhsT_scale=early_scales[:, 0:Q],
+                rhs=codes.bitcast(FP8X4), rhs_scale=scales, start=True, stop=True,
             )
             evac(staged[:], out_bank[:])
             nc.sync.dma_start(out[:, c0 * P : c0 * P + width], staged[:])
@@ -137,6 +137,11 @@ def tile_attend_residentset_kernel(tc, query, keys_words, keys_scales, size, val
         vr0 = resident(0, vals0, (at0, at0 + PIECE))
         a_step = tenant(at0, "a_step", FOUND, F32)
         look_up(a, a_step)
+        spread = turn.tile([P, PACK, P], F32, name="bank")
+        for t in range(PACK):
+            nc.tensor.transpose(spread[:, t, :], vsc_col[:, t : t + 1].to_broadcast([P, P]), ident[:])
+        vsc_row = tenant(at0 + PIECE, "vsc_row", FOUND, F32)
+        nc.scalar.copy(vsc_row[:].rearrange("m (k t) -> m k t", t=PACK), spread[:].rearrange("m t k -> m k t"))
         neg_s = own("neg_s", FOUND, F32)
         neg_max = own("neg_max", [P, 1], F32)
         p = own("p", FOUND, F32)
@@ -154,8 +159,8 @@ def tile_attend_residentset_kernel(tc, query, keys_words, keys_scales, size, val
         bank_w = turned(p_norm)
 
         vr1 = resident(1, vals1, (at1, at1 + PIECE))
-        woven01 = tenant(2 * SLOT, "woven01", [P, 2 * P, PACK], BF16)
-        weave(planes0, woven01[:, 0:P, :])
+        woven_w0 = tenant(2 * SLOT, "woven_w0", [P, 2 * P, PACK], BF16)
+        weave(planes0, woven_w0[:, P : 2 * P, :])
 
         vr2 = own("vr2", [P, R], F32)
         picked2_0 = tenant(at2, "picked2_0", [P, HALF], F32)
@@ -166,8 +171,7 @@ def tile_attend_residentset_kernel(tc, query, keys_words, keys_scales, size, val
         planes_w = tenant(3 * SLOT, "planes_w", PLANES, BF16)
         scale(bank_w, size_col, planes_w)
         nc.scalar.activation(vr2[:, halves[1]], picked2_1[:], ACT.Relu)
-        woven_w = own("woven_w", WOVEN, BF16)
-        weave(planes_w, woven_w[:])
+        weave(planes_w, woven_w0[:, 0:P, :])
 
         vt1 = tenant(at2 - PIECE // 2, "vt1", FOUND, F32)
         look_up(vr1, vt1)
@@ -176,35 +180,42 @@ def tile_attend_residentset_kernel(tc, query, keys_words, keys_scales, size, val
         vr3 = resident(3, vals3, (at2 + PIECE // 2, at3))
         planes1 = tenant(4 * SLOT, "planes1", PLANES, BF16)
         scale(bank1, vsc_col, planes1)
-        weave(planes1, woven01[:, P : 2 * P, :])
+        woven1 = own("woven1", WOVEN, BF16)
+        weave(planes1, woven1[:])
         vt2 = tenant(at2 + PIECE // 2, "vt2", FOUND, F32)
         look_up(vr2, vt2)
-        vt3 = own("vt3", FOUND, F32)
-        look_up(vr3, vt3)
+        at4 = at3 + 2 * PIECE
+        vv3 = tenant(at4 + 2 * PIECE, "vv3", FOUND, BF16)
+        vt3 = [tenant(at4, "vt3_0", [P, I // 2], F32), own("vt3_1", [P, I // 2], F32)]
+        for h in range(2):
+            nc.vector.tensor_copy(vt3[h][:], vr3[:].indirect(idx2[:, h * I // 32 : (h + 1) * I // 32]))
+        for h in range(2):
+            slots = slice(h * I // 2, (h + 1) * I // 2)
+            nc.vector.tensor_tensor(vv3[:, slots], vt3[h][:], vsc_row[:, slots], ALU.mult)
 
-        w_codes = tenant(at3, "w_codes", [P, Q], U32)
-        w_scales = own("w_scales", [P, Q], U8)
-        quantise(woven_w, w_codes, w_scales)
-        codes01 = tenant(at3 + 4 * Q, "codes01", [P, 2 * P], U32)
-        scales01 = own("scales01", [P, 2 * P], U8)
-        quantise(woven01, codes01, scales01)
+        bank2 = turned(vt2)
+        bank3 = turn.tile([P, 2, P], F32, name="bank")
+        pairs = vv3[:].bitcast(F32)
+        for u in range(2):
+            nc.tensor.transpose(bank3[:, u, :], pairs[:, u : I // 2 : 2], ident[:])
 
-        woven2 = own("woven2", WOVEN, BF16)
-        planes2 = own("planes2", PLANES, BF16)
-        scale(turned(vt2), vsc_col, planes2)
-        weave(planes2, woven2[:])
-        bank3 = turned(vt3)
-        product(0, codes01, scales01, nc.scalar.copy)
+        woven2 = tenant(at4 + PIECE // 4, "woven2", WOVEN, BF16)
+        nc.vector.tensor_tensor(
+            woven2[:], bank2[:].rearrange("p t n -> p n t"), vsc_col[:].unsqueeze(1).to_broadcast([P, P, PACK]), ALU.mult
+        )
+        early_codes = tenant(at4 + PIECE // 4 - 4 * (Q + 2 * P), "early_codes", [P, Q + 2 * P], U32)
+        early_scales = own("early_scales", [P, Q + 2 * P], U8)
+        quantise(woven_w0, early_codes[:, 0 : Q + P], early_scales[:, 0 : Q + P])
+        quantise(woven2, early_codes[:, Q + P :], early_scales[:, Q + P :])
+        product(0, early_codes[:, Q:], early_scales[:, Q:], nc.scalar.copy)
 
         woven3 = own("woven3", WOVEN, BF16)
-        nc.vector.tensor_tensor(
-            woven3[:], bank3[:].rearrange("p t n -> p n t"), vsc_col[:].unsqueeze(1).to_broadcast([P, P, PACK]), ALU.mult
-        )
-        codes2 = own("codes2", [P, P], U32)
-        scales2 = own("scales2", [P, P], U8)
-        quantise(woven2, codes2, scales2)
+        nc.vector.tensor_copy(woven3[:].bitcast(F32), bank3[:].rearrange("p u n -> p n u"))
+        codes1 = tenant(at4 + 2 * PIECE, "codes1", [P, P], U32)
+        scales1 = own("scales1", [P, P], U8)
+        quantise(woven1, codes1[:], scales1[:])
         codes3 = own("codes3", [P, P], U32)
         scales3 = own("scales3", [P, P], U8)
-        quantise(woven3, codes3, scales3)
-        product(2, codes2, scales2, nc.scalar.copy)
-        product(3, codes3, scales3, nc.vector.tensor_copy)
+        quantise(woven3, codes3[:], scales3[:])
+        product(2, codes1[:], scales1[:], nc.scalar.copy)
+        product(3, codes3[:], scales3[:], nc.vector.tensor_copy)

@@ -53,7 +53,8 @@ def tile_attend_residentset_kernel(tc, query, keys_words, keys_scales, size, val
         nc.sync.dma_start(q_raw[:], query.rearrange("(p t) q -> p t q", t=PACK))
         nc.sync.dma_start(idx2[:], offs2)
         for g in range(4):
-            nc.sync.dma_start(key_bytes[32 * g : 32 * g + 4, :].bitcast(I32), keys_scales[0, 4 * g : 4 * g + 4, :].bitcast(I32))
+            queue = nc.sync if g % 2 == 0 else nc.scalar
+            queue.dma_start(key_bytes[32 * g : 32 * g + 4, :].bitcast(I32), keys_scales[0, 4 * g : 4 * g + 4, :].bitcast(I32))
         key_words = tenant(0, "key_words", [P, T], U32)
         nc.sync.dma_start(key_words[:].bitcast(I32), keys_words[0].rearrange("p n t -> p (n t)").bitcast(I32))
 
@@ -92,12 +93,12 @@ def tile_attend_residentset_kernel(tc, query, keys_words, keys_scales, size, val
         vals2 = load_vals(1, 3 * SLOT)
         vals3 = load_vals(3, 4 * SLOT)
 
-        def resident(c, pool_rows, places):
+        def resident(c, pool_rows, places, cut):
             vr = own("vr%d" % c, [P, R], F32)
-            for h in range(2):
-                picked = tenant(places[h], "picked%d_%d" % (c, h), [P, HALF], F32)
-                nc.vector.tensor_copy(picked[:], pool_rows[:].indirect(idx_halves[h]))
-                nc.scalar.activation(vr[:, halves[h]], picked[:], ACT.Relu)
+            for h, (lo, hi) in enumerate(((0, cut), (cut, R))):
+                picked = tenant(places[h], "picked%d_%d" % (c, h), [P, hi - lo], F32)
+                nc.vector.tensor_copy(picked[:], pool_rows[:].indirect(idx[:, lo // 16 : hi // 16]))
+                nc.scalar.activation(vr[:, lo:hi], picked[:], ACT.Relu)
             return vr
 
         def look_up(window, found):
@@ -132,9 +133,9 @@ def tile_attend_residentset_kernel(tc, query, keys_words, keys_scales, size, val
 
         FOUND, PLANES, WOVEN = [P, I], [P, PACK, P], [P, P, PACK]
         base = 5 * SLOT
-        at0, at1, at2, at3 = base, base + 2 * PIECE, base + 5 * PIECE, base + 8 * PIECE
+        at0, at1, at2, at3 = base, base + 3 * PIECE, base + 6 * PIECE, base + 8 * PIECE
 
-        vr0 = resident(0, vals0, (at0, at0 + PIECE))
+        vr0 = resident(0, vals0, (at0, at0 + PIECE), R // 4)
         a_step = tenant(at0, "a_step", FOUND, F32)
         look_up(a, a_step)
         spread = turn.tile([P, PACK, P], F32, name="bank")
@@ -158,9 +159,7 @@ def tile_attend_residentset_kernel(tc, query, keys_words, keys_scales, size, val
         scale(turned(vt0), vsc_col, planes0)
         bank_w = turned(p_norm)
 
-        vr1 = resident(1, vals1, (at1, at1 + PIECE))
-        woven_w0 = tenant(2 * SLOT, "woven_w0", [P, 2 * P, PACK], BF16)
-        weave(planes0, woven_w0[:, P : 2 * P, :])
+        vr1 = resident(1, vals1, (at1, at1 + PIECE), HALF)
 
         vr2 = own("vr2", [P, R], F32)
         picked2_0 = tenant(at2, "picked2_0", [P, HALF], F32)
@@ -168,16 +167,19 @@ def tile_attend_residentset_kernel(tc, query, keys_words, keys_scales, size, val
         nc.vector.tensor_copy(picked2_0[:], vals2[:].indirect(idx_halves[0]))
         nc.scalar.activation(vr2[:, halves[0]], picked2_0[:], ACT.Relu)
         nc.vector.tensor_copy(picked2_1[:], vals2[:].indirect(idx_halves[1]))
+        woven0 = tenant(3 * SLOT + PIECE, "woven0", WOVEN, BF16)
+        weave(planes0, woven0[:])
         planes_w = tenant(3 * SLOT, "planes_w", PLANES, BF16)
         scale(bank_w, size_col, planes_w)
         nc.scalar.activation(vr2[:, halves[1]], picked2_1[:], ACT.Relu)
-        weave(planes_w, woven_w0[:, 0:P, :])
 
         vt1 = tenant(at2 - PIECE // 2, "vt1", FOUND, F32)
         look_up(vr1, vt1)
         bank1 = turned(vt1)
 
-        vr3 = resident(3, vals3, (at2 + PIECE // 2, at3))
+        vr3 = resident(3, vals3, (at2 + PIECE // 2, at3), HALF)
+        woven_w = tenant(4 * SLOT + PIECE, "woven_w", WOVEN, BF16)
+        weave(planes_w, woven_w[:])
         planes1 = tenant(4 * SLOT, "planes1", PLANES, BF16)
         scale(bank1, vsc_col, planes1)
         woven1 = own("woven1", WOVEN, BF16)
@@ -205,12 +207,13 @@ def tile_attend_residentset_kernel(tc, query, keys_words, keys_scales, size, val
         )
         early_codes = tenant(at4 + PIECE // 4 - 4 * (Q + 2 * P), "early_codes", [P, Q + 2 * P], U32)
         early_scales = own("early_scales", [P, Q + 2 * P], U8)
-        quantise(woven_w0, early_codes[:, 0 : Q + P], early_scales[:, 0 : Q + P])
+        quantise(woven_w, early_codes[:, 0:Q], early_scales[:, 0:Q])
+        quantise(woven0, early_codes[:, Q : Q + P], early_scales[:, Q : Q + P])
         quantise(woven2, early_codes[:, Q + P :], early_scales[:, Q + P :])
-        product(0, early_codes[:, Q:], early_scales[:, Q:], nc.scalar.copy)
 
         woven3 = own("woven3", WOVEN, BF16)
-        nc.vector.tensor_copy(woven3[:].bitcast(F32), bank3[:].rearrange("p u n -> p n u"))
+        nc.scalar.copy(woven3[:].bitcast(F32), bank3[:].rearrange("p u n -> p n u"))
+        product(0, early_codes[:, Q:], early_scales[:, Q:], nc.scalar.copy)
         codes1 = tenant(at4 + 2 * PIECE, "codes1", [P, P], U32)
         scales1 = own("scales1", [P, P], U8)
         quantise(woven1, codes1[:], scales1[:])

from contextlib import ExitStack

import concourse.mybir as mybir

D, T, R, I, Q, E = 512, 2048, 1024, 512, 128, 512
FLOPS = 2 * D * Q * R + 2 * I * Q * E

F32 = mybir.dt.float32
BF16 = mybir.dt.bfloat16
I32 = mybir.dt.int32
U32 = mybir.dt.uint32
U16 = mybir.dt.uint16
U8 = mybir.dt.uint8
FP8X4 = mybir.dt.float8_e4m3fn_x4
ALU = mybir.AluOpType
ACT = mybir.ActivationFunctionType

P = 128
PACK = 4
BANK = 512
SLOT = 4 * T
HALF = R // 2
PIECE = 4 * HALF


def tile_attend_residentset_kernel(tc, query, keys_words, keys_scales, size, vals, vsc, offs, offs2, out):
    nc = tc.nc
    with ExitStack() as ctx:
        keep = ctx.enter_context(tc.tile_pool(name="keep", bufs=1))
        shared = ctx.enter_context(tc.tile_pool(name="shared", bufs=1))
        psum = ctx.enter_context(tc.psum_pool(name="psum", bufs=1))
        turn = ctx.enter_context(tc.psum_pool(name="turn", bufs=3))

        def tenant(at, name, shape, dtype):
            return shared.tile(shape, dtype, name=name, offset=at, align_bytes=64)

        def own(name, shape, dtype):
            return keep.tile(shape, dtype, name=name, align_bytes=64)

        idx = keep.tile([P, R // 16], U16, name="idx")
        idx2 = keep.tile([P, I // 16], U16, name="idx2")
        ident = own("ident", [P, P], F32)
        key_bytes = own("key_bytes", [P, T], U8)
        ones = tenant(SLOT - 256, "ones", [P, P], F32)
        q_raw = own("q_raw", [P, PACK, Q], F32)

        nc.vector.memset(key_bytes[:].bitcast(I32), 0)
        nc.vector.memset(ones[:], 1.0)
        nc.gpsimd.affine_select(
            out=ident[:], in_=ones[:], compare_op=ALU.is_equal, fill=0.0, base=0, pattern=[[-1, P]], channel_multiplier=1
        )
        nc.sync.dma_start(idx[:], offs)
        nc.sync.dma_start(q_raw[:], query.rearrange("(p t) q -> p t q", t=PACK))
        nc.sync.dma_start(idx2[:], offs2)
        for g in range(4):
            queue = nc.sync if g % 2 == 0 else nc.scalar
            queue.dma_start(key_bytes[32 * g : 32 * g + 4, :].bitcast(I32), keys_scales[0, 4 * g : 4 * g + 4, :].bitcast(I32))
        key_words = tenant(0, "key_words", [P, T], U32)
        nc.sync.dma_start(key_words[:].bitcast(I32), keys_words[0].rearrange("p n t -> p (n t)").bitcast(I32))

        def load_vals(c, slot):
            pool_rows = tenant(slot, "vals%d" % c, [P, T], F32)
            nc.sync.dma_start(pool_rows[:], vals[c * P : (c + 1) * P, :])
            return pool_rows

        vals0 = load_vals(0, SLOT)
        q_bf = own("q_bf", [P, Q, PACK], BF16)
        q_codes = tenant(4 * SLOT, "q_codes", [P, Q], U32)
        q_scales = own("q_scales", [P, Q], U8)
        nc.scalar.copy(q_bf[:], q_raw[:].rearrange("p t q -> p q t"))

        halves = [slice(h * HALF, (h + 1) * HALF) for h in range(2)]
        idx_halves = [idx[:, h * HALF // 16 : (h + 1) * HALF // 16] for h in range(2)]

        kg_words = tenant(2 * SLOT, "kg_words", [P, R], U32)
        kg_bytes = tenant(3 * SLOT, "kg_bytes", [P, R], U8)
        nc.vector.tensor_copy(kg_bytes[:], key_bytes[:].indirect(idx[:]))
        nc.vector.quantize_mx(out=q_codes[:].bitcast(FP8X4), scales=q_scales[:], in_=q_bf[:].rearrange("p q t -> p (q t)"))
        a = own("a", [P, R], F32)
        for h in range(2):
            nc.vector.tensor_copy(kg_words[:, halves[h]], key_words[:].indirect(idx_halves[h]))
            score_bank = psum.tile([P, HALF], F32, name="score_bank%d" % h)
            nc.tensor.matmul_mx(
                out=score_bank[:], lhsT=q_codes[:].bitcast(FP8X4), lhsT_scale=q_scales[:],
                rhs=kg_words[:, halves[h]].bitcast(FP8X4), rhs_scale=kg_bytes[:, halves[h]], start=True, stop=True,
            )
            nc.scalar.copy(a[:, halves[h]], score_bank[:])
        vsc_col = tenant(0, "vsc_col", [P, PACK], F32)
        nc.sync.dma_start(vsc_col[:], vsc.rearrange("(p t) o -> p (t o)", t=PACK))
        size_col = tenant(64, "size_col", [P, PACK], F32)
        nc.sync.dma_start(size_col[:], size.rearrange("o (p t) -> (o p) t", t=PACK))
        vals1 = load_vals(2, 2 * SLOT)
        vals2 = load_vals(1, 3 * SLOT)
        vals3 = load_vals(3, 4 * SLOT)

        def resident(c, pool_rows, places, cut):
            vr = own("vr%d" % c, [P, R], F32)
            for h, (lo, hi) in enumerate(((0, cut), (cut, R))):
                picked = tenant(places[h], "picked%d_%d" % (c, h), [P, hi - lo], F32)
                nc.vector.tensor_copy(picked[:], pool_rows[:].indirect(idx[:, lo // 16 : hi // 16]))
                nc.scalar.activation(vr[:, lo:hi], picked[:], ACT.Relu)
            return vr

        def look_up(window, found):
            nc.vector.tensor_copy(found[:], window[:].indirect(idx2[:]))

        def turned(rows):
            bank = turn.tile([P, PACK, P], F32, name="bank")
            for t in range(PACK):
                nc.tensor.transpose(bank[:, t, :], rows[:, t : I : PACK], ident[:])
            return bank

        def scale(bank, factor, planes):
            for t in range(PACK):
                nc.scalar.activation(planes[:, t, :], bank[:, t, :], ACT.Copy, scale=factor[:, t : t + 1])

        def weave(planes, woven):
            nc.scalar.copy(woven, planes[:].rearrange("p t n -> p n t"))

        def quantise(woven, codes, scales):
            nc.vector.quantize_mx(out=codes.bitcast(FP8X4), scales=scales, in_=woven[:].rearrange("p n t -> p (n t)"))

        def product(c0, codes, scales, evac):
            width = codes.shape[1]
            out_bank = psum.tile([P, width], F32, name="out_bank%d" % c0)
            staged = own("staged%d" % c0, [P, width], F32)
            nc.tensor.matmul_mx(
                out=out_bank[:], lhsT=early_codes[:, 0:Q].bitcast(FP8X4), lhsT_scale=early_scales[:, 0:Q],
                rhs=codes.bitcast(FP8X4), rhs_scale=scales, start=True, stop=True,
            )
            evac(staged[:], out_bank[:])
            nc.sync.dma_start(out[:, c0 * P : c0 * P + width], staged[:])

        FOUND, PLANES, WOVEN = [P, I], [P, PACK, P], [P, P, PACK]
        base = 5 * SLOT
        at0, at1, at2, at3 = base, base + 3 * PIECE, base + 6 * PIECE, base + 8 * PIECE

        vr0 = resident(0, vals0, (at0, at0 + PIECE), R // 4)
        a_step = tenant(at0, "a_step", FOUND, F32)
        look_up(a, a_step)
        spread = turn.tile([P, PACK, P], F32, name="bank")
        for t in range(PACK):
            nc.tensor.transpose(spread[:, t, :], vsc_col[:, t : t + 1].to_broadcast([P, P]), ident[:])
        vsc_row = tenant(at0 + PIECE, "vsc_row", FOUND, F32)
        nc.scalar.copy(vsc_row[:].rearrange("m (k t) -> m k t", t=PACK), spread[:].rearrange("m t k -> m k t"))
        neg_s = own("neg_s", FOUND, F32)
        neg_max = own("neg_max", [P, 1], F32)
        p = own("p", FOUND, F32)
        p_sum = own("p_sum", [P, 1], F32)
        nc.vector.tensor_scalar(neg_s[:], a_step[:], -1.5, None, ALU.mult, ALU.min, accum_out=neg_max[:])
        nc.scalar.activation(p[:], neg_s[:], ACT.Exp, bias=neg_max[:], scale=-1.0, accum_out=p_sum[:])
        vt0 = own("vt0", FOUND, F32)
        look_up(vr0, vt0)
        inv_sum = own("inv_sum", [P, 1], F32)
        nc.vector.reciprocal(inv_sum[:], p_sum[:])
        p_norm = own("p_norm", FOUND, F32)
        nc.scalar.activation(p_norm[:], p[:], ACT.Copy, scale=inv_sum[:])
        planes0 = own("planes0", PLANES, BF16)
        scale(turned(vt0), vsc_col, planes0)
        bank_w = turned(p_norm)

        vr1 = resident(1, vals1, (at1, at1 + PIECE), HALF)

        vr2 = own("vr2", [P, R], F32)
        picked2_0 = tenant(at2, "picked2_0", [P, HALF], F32)
        picked2_1 = own("picked2_1", [P, HALF], F32)
        nc.vector.tensor_copy(picked2_0[:], vals2[:].indirect(idx_halves[0]))
        nc.scalar.activation(vr2[:, halves[0]], picked2_0[:], ACT.Relu)
        nc.vector.tensor_copy(picked2_1[:], vals2[:].indirect(idx_halves[1]))
        woven0 = tenant(3 * SLOT + PIECE, "woven0", WOVEN, BF16)
        weave(planes0, woven0[:])
        planes_w = tenant(3 * SLOT, "planes_w", PLANES, BF16)
        scale(bank_w, size_col, planes_w)
        nc.scalar.activation(vr2[:, halves[1]], picked2_1[:], ACT.Relu)

        vt1 = tenant(at2 - PIECE // 2, "vt1", FOUND, F32)
        look_up(vr1, vt1)
        bank1 = turned(vt1)

        vr3 = resident(3, vals3, (at2 + PIECE // 2, at3), HALF)
        woven_w = tenant(4 * SLOT + PIECE, "woven_w", WOVEN, BF16)
        weave(planes_w, woven_w[:])
        planes1 = tenant(4 * SLOT, "planes1", PLANES, BF16)
        scale(bank1, vsc_col, planes1)
        woven1 = own("woven1", WOVEN, BF16)
        weave(planes1, woven1[:])
        vt2 = tenant(at2 + PIECE // 2, "vt2", FOUND, F32)
        look_up(vr2, vt2)
        at4 = at3 + 2 * PIECE
        vv3 = tenant(at4 + 2 * PIECE, "vv3", FOUND, BF16)
        vt3 = [tenant(at4, "vt3_0", [P, I // 2], F32), own("vt3_1", [P, I // 2], F32)]
        for h in range(2):
            nc.vector.tensor_copy(vt3[h][:], vr3[:].indirect(idx2[:, h * I // 32 : (h + 1) * I // 32]))
        for h in range(2):
            slots = slice(h * I // 2, (h + 1) * I // 2)
            nc.vector.tensor_tensor(vv3[:, slots], vt3[h][:], vsc_row[:, slots], ALU.mult)

        bank2 = turned(vt2)
        bank3 = turn.tile([P, 2, P], F32, name="bank")
        pairs = vv3[:].bitcast(F32)
        for u in range(2):
            nc.tensor.transpose(bank3[:, u, :], pairs[:, u : I // 2 : 2], ident[:])

        woven2 = tenant(at4 + PIECE // 4, "woven2", WOVEN, BF16)
        nc.vector.tensor_tensor(
            woven2[:], bank2[:].rearrange("p t n -> p n t"), vsc_col[:].unsqueeze(1).to_broadcast([P, P, PACK]), ALU.mult
        )
        early_codes = tenant(at4 + PIECE // 4 - 4 * (Q + 2 * P), "early_codes", [P, Q + 2 * P], U32)
        early_scales = own("early_scales", [P, Q + 2 * P], U8)
        quantise(woven_w, early_codes[:, 0:Q], early_scales[:, 0:Q])
        quantise(woven0, early_codes[:, Q : Q + P], early_scales[:, Q : Q + P])
        quantise(woven2, early_codes[:, Q + P :], early_scales[:, Q + P :])

        woven3 = own("woven3", WOVEN, BF16)
        nc.scalar.copy(woven3[:].bitcast(F32), bank3[:].rearrange("p u n -> p n u"))
        product(0, early_codes[:, Q:], early_scales[:, Q:], nc.scalar.copy)
        codes1 = tenant(at4 + 2 * PIECE, "codes1", [P, P], U32)
        scales1 = own("scales1", [P, P], U8)
        quantise(woven1, codes1[:], scales1[:])
        codes3 = own("codes3", [P, P], U32)
        scales3 = own("scales3", [P, P], U8)
        quantise(woven3, codes3[:], scales3[:])
        product(2, codes1[:], scales1[:], nc.scalar.copy)
        product(3, codes3[:], scales3[:], nc.vector.tensor_copy)
